import numpy as np
import ml_dtypes


def mxq(x, axis, fmt="e4m3"):
    dtype, down = {"e4m3": (ml_dtypes.float8_e4m3fn, 7), "e5m2": (ml_dtypes.float8_e5m2, 14)}[fmt]
    v = np.moveaxis(np.asarray(x, np.float32).astype(ml_dtypes.bfloat16).astype(np.float64), axis, -1)
    blocks = v.reshape(v.shape[:-1] + (-1, 32))
    amax = np.abs(blocks).max(-1, keepdims=True)
    byte = np.maximum(np.where(amax > 0, np.frexp(amax)[1] - 1 + 127, 0) - down, 1)
    scale = np.exp2(byte - 127.0)
    codes = (blocks / scale).astype(np.float32).astype(dtype).astype(np.float64)
    return np.moveaxis((codes * scale).reshape(v.shape), -1, axis)


WIDE = False


def mx_kscale(k):
    if not WIDE:
        return np.ones(k)
    levels = np.array([10, -10, 5, -5, 0])
    if k % 512:
        return np.exp2(np.random.permutation(np.resize(levels, k // 32))).repeat(32)
    a = np.empty((k // 512, 16))
    for p in range(k // 512):
        a[p, :8] = np.random.permutation(np.resize(levels, 8))
        for g in range(8):
            far = levels[np.abs(levels - a[p, g]) >= 10]
            a[p, g + 8] = far[np.random.randint(len(far))]
    return np.exp2(a.ravel()).repeat(32)


def f64(x):
    return np.asarray(x).astype(np.float64)


def striped(idx):
    return np.tile(idx.reshape(-1, 16).T, (8, 1)).astype(np.uint16)


def unstriped(offs):
    return offs[:16].T.reshape(-1).astype(np.int64)


def striped8(idx):
    return np.concatenate([x.reshape(-1, 16).T for x in idx]).astype(np.uint16)


def runs(offs, k):
    lists = np.stack([offs[16 * r : 16 * r + 16].T.reshape(-1) for r in range(8)]).astype(np.int64)
    return lists[np.arange(k) % 512 // 64]


def pack_weight(w):
    k, n = w.shape
    w = f64(np.asarray(w, np.float32).astype(ml_dtypes.bfloat16)).reshape(k // 32, 32, n)
    amax = np.abs(w).max(1)
    byte = np.clip(np.where(amax > 0, np.frexp(amax)[1] - 1 + 127 - 7, 1), 1, 254)
    scaled = (w * np.exp2(127.0 - byte)[:, None, :]).reshape(k, n).astype(np.float32)
    words = np.ascontiguousarray(scaled.reshape(k // 512, 128, 4, n).transpose(0, 1, 3, 2)).astype(ml_dtypes.float8_e4m3fn).view(np.uint8)
    return words, np.ascontiguousarray(byte.astype(np.uint8).reshape(k // 512, 16, n))


def unpack_weight(words, scales):
    g, p, n, _ = words.shape
    vals = np.ascontiguousarray(words).view(ml_dtypes.float8_e4m3fn).astype(np.float64) * np.repeat(np.exp2(scales.astype(np.float64) - 127.0), 8, axis=1)[..., None]
    return vals.transpose(0, 1, 3, 2).reshape(g * 512, n)


def relu(v):
    return np.maximum(v, 0.0)


def sigmoid(v):
    return 1.0 / (1.0 + np.exp(-np.maximum(v, -700.0)))


K, T, S, V, H, U = 512, 2048, 512, 512, 512, 1024


def setup_inputs():
    n = np.random.standard_normal
    s = mx_kscale(K)[:, None]
    u = mx_kscale(S)
    packed_xT = pack_weight(n((K, T)) * s)
    return {
        "x_words": packed_xT[0],
        "x_scales": packed_xT[1],
        "w1": (n((K, H)) / np.sqrt(K) / s).astype(np.float32),
        "w2": (n((K, H)) / np.sqrt(K) / s).astype(np.float32),
        "ga": (np.random.uniform(0.5, 1.5, (H, 1)) * u[:, None]).astype(np.float32),
        "gb": (np.random.uniform(0.5, 1.5, (H, 1)) / u[:, None]).astype(np.float32),
        "offs": striped8(np.random.randint(0, T, (8, S))),
        "two": striped(np.random.permutation(T)[:V]),
        "n1": striped(np.random.permutation(S)),
        "n2": striped(np.random.permutation(S)),
        "n3": striped(np.random.permutation(V)),
        "n4": striped(np.random.permutation(V)),
        "n5": striped8(np.stack([np.random.permutation(U)[:V] for _ in range(8)])),
        "n6": striped8(np.stack([np.random.permutation(V) for _ in range(8)])),
    }


def reference(x_words, x_scales, w1, w2, ga, gb, offs, two, n1, n2, n3, n4, n5, n6):
    xq = unpack_weight(x_words, x_scales)[np.arange(K)[:, None], runs(offs, K)]
    a = mxq(f64(w1), 0, "e4m3").T @ xq
    z = f64(ga) * (np.maximum(a[:, unstriped(n1)], a[:, unstriped(n2)]) - (0.75 * a))
    x_two = unpack_weight(x_words, x_scales)[:, unstriped(two)]
    b = mxq(f64(w2), 0, "e4m3").T @ x_two
    st = b[:, unstriped(n3)] - b
    z2 = f64(gb) * (b * (sigmoid(st[:, unstriped(n4)])))
    s = 0.0625 * ((mxq(z, 0, "e4m3").T @ mxq(z2, 0, "e4m3")))
    nw = s - (relu(s[np.arange(S)[:, None], runs(n6, S)]))
    out = np.zeros((S, U))
    out[np.arange(S)[:, None], runs(n5, S)] = nw
    return out

@@ -1,0 +1,221 @@
+from contextlib import ExitStack
+
+import concourse.mybir as mybir
+
+F32 = mybir.dt.float32
+BF16 = mybir.dt.bfloat16
+I32 = mybir.dt.int32
+U32 = mybir.dt.uint32
+U16 = mybir.dt.uint16
+U8 = mybir.dt.uint8
+FP8X4 = mybir.dt.float8_e4m3fn_x4
+ALU = mybir.AluOpType
+ACT = mybir.ActivationFunctionType
+
+P = 128
+PACK = 4
+K, T, S, V, H, U = 512, 2048, 512, 512, 512, 1024
+HALF = 256
+FLOPS = 3 * 2 * 512 * 512 * 512
+
+
+def tile_picked_hkqoverhopdpagez_none_p_kernel(tc, x_words, x_scales, w1, w2, ga, gb, offs, two, n1, n2, n3, n4, n5, n6, out):
+    nc = tc.nc
+    with ExitStack() as ctx:
+        keep = ctx.enter_context(tc.tile_pool(name="keep", bufs=1))
+        psum = ctx.enter_context(tc.psum_pool(name="psum", bufs=1))
+
+        def tile(shape, dtype, name):
+            return keep.tile(shape, dtype, name=name, align_bytes=64)
+
+        def load_list(src, name):
+            t = keep.tile([P, S // 16], U16, name=name)
+            nc.sync.dma_start(t[:], src)
+            return t
+
+        def half(lst, h):
+            return lst[:, 16 * h : 16 * (h + 1)]
+
+        def cols(h):
+            return slice(HALF * h, HALF * (h + 1))
+
+        xs = tile([P, T], U8, "xs")
+        nc.gpsimd.memset(xs[:].bitcast(I32), 0)
+        pages = [tile([P, U], F32, f"page{u}") for u in range(PACK)]
+
+        for q in range(4):
+            nc.sync.dma_start(xs[32 * q : 32 * q + 4, :].bitcast(I32), x_scales[0, 4 * q : 4 * q + 4, :].bitcast(I32))
+        by_row = x_scales[0].rearrange("(q r) n -> r q n", r=4)
+        for r in (2, 3):
+            nc.gpsimd.dma_start(xs[14 + r : P : 32, :].bitcast(I32), by_row[r].bitcast(I32))
+        two_l = load_list(two, "two_l")
+        offs_l = load_list(offs, "offs_l")
+        xw = tile([P, T], U32, "xw")
+        nc.sync.dma_start(xw[:].bitcast(I32), x_words[0].rearrange("p n t -> p (n t)").bitcast(I32))
+        w2_raw = tile([P, PACK, H], F32, "w2_raw")
+        nc.sync.dma_start(w2_raw[:], w2.rearrange("(p j) c -> p j c", j=PACK))
+        ga_t = tile([P, PACK], F32, "ga_t")
+        gb_t = tile([P, PACK], F32, "gb_t")
+        nc.gpsimd.dma_start(ga_t[:], ga.rearrange("(p t) o -> p (t o)", t=PACK))
+        nc.gpsimd.dma_start(gb_t[:], gb.rearrange("(p t) o -> p (t o)", t=PACK))
+        n3_l = load_list(n3, "n3_l")
+        n4_l = load_list(n4, "n4_l")
+        n1_l = load_list(n1, "n1_l")
+        n2_l = load_list(n2, "n2_l")
+        w1_raw = tile([P, PACK, H], F32, "w1_raw")
+        nc.sync.dma_start(w1_raw[:], w1.rearrange("(p j) c -> p j c", j=PACK))
+        n6_l = load_list(n6, "n6_l")
+        n5_l = load_list(n5, "n5_l")
+
+        for u in range(PACK):
+            (nc.vector if u < 2 else nc.gpsimd).memset(pages[u][:].bitcast(I32), 0)
+
+        ga_abs = tile([P, PACK], F32, "ga_abs")
+        pos2 = tile([P, PACK], F32, "pos2")
+        sgn = tile([P, PACK], F32, "sgn")
+        gb_s = tile([P, PACK], F32, "gb_s")
+        own = tile([P, PACK], F32, "own")
+        nc.gpsimd.tensor_scalar(pos2[:], ga_t[:], 0.0, 2.0, ALU.is_ge, ALU.mult)
+        nc.gpsimd.tensor_scalar(sgn[:], pos2[:], 1.0, -1.0, ALU.mult, ALU.add)
+        nc.gpsimd.tensor_tensor(ga_abs[:], ga_t[:], sgn[:], ALU.mult)
+        nc.gpsimd.tensor_tensor(gb_s[:], gb_t[:], sgn[:], ALU.mult)
+        nc.gpsimd.tensor_scalar(own[:], ga_abs[:], -0.75, 0.0, ALU.mult, ALU.add)
+
+        two_s = tile([P, V], U8, "two_s")
+        nc.vector.tensor_copy(two_s[:], xs[:].indirect(two_l[:]))
+        offs_s = tile([P, S], U8, "offs_s")
+        nc.vector.tensor_copy(offs_s[:], xs[:].indirect(offs_l[:]))
+        a_s = tile([P, S], U8, "a_s")
+        nc.vector.tensor_copy(a_s[:].bitcast(I32), offs_s[:].bitcast(I32))
+        for r in (2, 3):
+            nc.sync.dma_start(a_s[r:P:32, :].bitcast(I32), offs_s[14 + r : P : 32, :].bitcast(I32))
+
+        two_w = tile([P, V], U32, "two_w")
+        nc.vector.tensor_copy(two_w[:], xw[:].indirect(two_l[:]))
+        offs_w = tile([P, S], U32, "offs_w")
+        nc.vector.tensor_copy(offs_w[:], xw[:].indirect(offs_l[:]))
+
+        def cast_pair(raw, u, name, copy):
+            grouped = tile([P, 2, P, PACK], BF16, name)
+            copy(grouped[:].rearrange("p t m j -> p m j t"), raw[:].rearrange("p j (m t) -> p m j t", t=PACK)[:, :, :, 2 * u : 2 * u + 2])
+            return grouped
+
+        def quantize(flat, width, name):
+            codes = tile([P, width], U32, name + "_c")
+            scales = tile([P, width], U8, name + "_s")
+            nc.vector.quantize_mx(out=codes[:].bitcast(FP8X4), scales=scales[:], in_=flat)
+            return codes, scales
+
+        def product(bank, lhs, c, rhs):
+            nc.tensor.matmul_mx(out=bank[:], lhsT=lhs[0][:, P * c : P * (c + 1)].bitcast(FP8X4), lhsT_scale=lhs[1][:, P * c : P * (c + 1)],
+                                rhs=rhs[0][:].bitcast(FP8X4), rhs_scale=rhs[1][:], start=True, stop=True)
+
+        w2_g = [cast_pair(w2_raw, u, f"w2_g{u}", nc.vector.tensor_copy if u == 0 else lambda o, i: nc.scalar.activation(o, i, ACT.Copy)) for u in range(2)]
+        w2_q = [quantize(w2_g[u][:].rearrange("p t m j -> p (t m j)"), 2 * P, f"w2_q{u}") for u in range(2)]
+        b_ps = [psum.tile([P, V], F32, name=f"b_ps{t}", tag=f"bank{t}") for t in range(PACK)]
+        for t in range(PACK):
+            product(b_ps[t], w2_q[t // 2], t % 2, (two_w, two_s))
+
+        b_win = [tile([P, V], F32, f"b_win{t}") for t in range(PACK)]
+        b_own = [tile([P, V], F32, f"b_own{t}") for t in range(PACK)]
+        for t in range(PACK):
+            nc.scalar.copy(b_win[t][:], b_ps[t][:])
+            nc.sync.dma_start(b_own[t][:], b_win[t][:])
+
+        w1_g = [cast_pair(w1_raw, u, f"w1_g{u}", nc.vector.tensor_copy) for u in range(2)]
+        w1_q = [quantize(w1_g[u][:].rearrange("p t m j -> p (t m j)"), 2 * P, f"w1_q{u}") for u in range(2)]
+        a_ps = [psum.tile([P, S], F32, name=f"a_ps{t}", tag=f"bank{4 + t}") for t in range(PACK)]
+        for t in range(PACK):
+            product(a_ps[t], w1_q[t // 2], t % 2, (offs_w, a_s))
+
+        st = [tile([P, V], F32, f"st{t}") for t in range(PACK)]
+        sig = [tile([P, V], F32, f"sig{t}") for t in range(PACK)]
+        a_win = [tile([P, S], F32, f"a_win{t}") for t in range(PACK)]
+        g1 = [tile([P, S], F32, f"g1_{t}") for t in range(PACK)]
+        g2 = [tile([P, S], F32, f"g2_{t}") for t in range(PACK)]
+        big = [tile([P, S], F32, f"big{t}") for t in range(PACK)]
+        z_rows = tile([P, PACK, S], BF16, "z_rows")
+        z2_rows = tile([P, PACK, V], BF16, "z2_rows")
+
+        def a_evac(t):
+            nc.scalar.activation(a_win[t][:], a_ps[t][:], ACT.Copy, scale=ga_abs[:, t : t + 1])
+
+        def a_fetch(t, dst, lst, on_vector):
+            for h in range(2):
+                if on_vector:
+                    nc.vector.tensor_copy(dst[t][:, cols(h)], a_win[t][:].indirect(half(lst, h)))
+                else:
+                    nc.scalar.activation(dst[t][:, cols(h)], a_win[t][:].indirect(half(lst, h)), ACT.Copy)
+
+        def a_max(t, h):
+            nc.vector.tensor_tensor(big[t][:].rearrange("p (u m) -> p m u", u=PACK)[:, 64 * h : 64 * (h + 1), :],
+                                    g1[t][:, cols(h)].rearrange("p (m u) -> p m u", u=PACK),
+                                    g2[t][:, cols(h)].rearrange("p (m u) -> p m u", u=PACK), ALU.max)
+
+        def a_finish(t, u0, u1):
+            nc.vector.scalar_tensor_tensor(z_rows[:, t, :].rearrange("p (u m) -> p u m", u=PACK)[:, u0:u1, :],
+                                           a_ps[t][:].rearrange("p (m u) -> p u m", u=PACK)[:, u0:u1, :],
+                                           own[:, t : t + 1], big[t][:].rearrange("p (u m) -> p u m", u=PACK)[:, u0:u1, :], ALU.mult, ALU.add)
+
+        def interleave(rows, width, name, copy):
+            grouped = tile([P, width, PACK], BF16, name)
+            copy(grouped[:].rearrange("p (c i) t -> p c t i", i=4), rows.rearrange("p t (c i) -> p c t i", i=4))
+            return grouped
+
+        def b_sub(t):
+            for h in range(2):
+                nc.vector.tensor_tensor(st[t][:, cols(h)], b_win[t][:].indirect(half(n3_l, h)), b_own[t][:, cols(h)], ALU.subtract)
+
+        def b_finish(t):
+            for h in range(2):
+                nc.scalar.activation(sig[t][:, cols(h)], st[t][:].indirect(half(n4_l, h)), ACT.Sigmoid)
+            nc.vector.scalar_tensor_tensor(z2_rows[:, t, :], sig[t][:], gb_s[:, t : t + 1], b_ps[t][:], ALU.mult, ALU.mult)
+
+        def a_tile(t):
+            a_fetch(t, g1, n1_l, t == PACK - 1)
+            a_fetch(t, g2, n2_l, False)
+            for h in range(2):
+                a_max(t, h)
+            a_finish(t, 0, PACK if t < PACK - 1 else 1)
+
+        for t in range(PACK):
+            b_sub(t)
+        a_evac(0)
+        a_tile(0)
+        b_finish(0)
+        b_finish(1)
+        a_evac(1)
+        a_evac(3)
+        a_tile(1)
+        b_finish(2)
+        b_finish(3)
+        z2_g = interleave(z2_rows[:], V, "z2_g", nc.vector.tensor_copy)
+        z2_q = quantize(z2_g[:].rearrange("p c t -> p (c t)"), V, "z2_q")
+        a_evac(2)
+        a_tile(2)
+        a_tile(3)
+
+        z_g0 = interleave(z_rows[:, :, 0:P], P, "z_g0", nc.vector.tensor_copy)
+        z_q0 = quantize(z_g0[:].rearrange("p c t -> p (c t)"), P, "z_q0")
+        s_ps = [psum.tile([P, V], F32, name=f"s_ps{u}", tag=f"bank{u}") for u in range(PACK)]
+        product(s_ps[0], z_q0, 0, z2_q)
+        a_finish(PACK - 1, 1, PACK)
+        z_g1 = interleave(z_rows[:, :, P:S], S - P, "z_g1", nc.vector.tensor_copy)
+        z_q1 = quantize(z_g1[:].rearrange("p c t -> p (c t)"), S - P, "z_q1")
+        for u in range(1, PACK):
+            product(s_ps[u], z_q1, u - 1, z2_q)
+
+        out_rows = out.rearrange("(p u) w -> u p w", u=PACK)
+        for u in range(PACK):
+            pos = tile([P, V], F32, f"pos{u}")
+            nc.scalar.activation(pos[:], s_ps[u][:], ACT.Relu, scale=0.0625)
+            s_own = tile([P, V], F32, f"s_own{u}")
+            if u == 0:
+                nc.vector.tensor_scalar(s_own[:], s_ps[u][:], 0.0625, None, ALU.mult)
+            neg = tile([P, V], F32, f"neg{u}")
+            for h in range(2):
+                nc.scalar.activation(neg[:, cols(h)], pos[:].indirect(half(n6_l, h)), ACT.Copy, scale=-1.0)
+            if u > 0:
+                nc.scalar.activation(s_own[:], s_ps[u][:], ACT.Copy, scale=0.0625)
+            nc.vector.tensor_tensor(pages[u][:].indirect(n5_l[:]), s_own[:], neg[:], ALU.add)
+            nc.sync.dma_start(out_rows[u], pages[u][:])

@@ -25,8 +25,8 @@ def tile_picked_hkqoverhopdpagez_none_p_kernel(tc, x_words, x_scales, w1, w2, ga
         keep = ctx.enter_context(tc.tile_pool(name="keep", bufs=1))
         psum = ctx.enter_context(tc.psum_pool(name="psum", bufs=1))
 
-        def tile(shape, dtype, name):
-            return keep.tile(shape, dtype, name=name, align_bytes=64)
+        def tile(shape, dtype, name, tag=None):
+            return keep.tile(shape, dtype, name=name, tag=tag or name, align_bytes=64)
 
         def load_list(src, name):
             t = keep.tile([P, S // 16], U16, name=name)
@@ -40,14 +40,11 @@ def tile_picked_hkqoverhopdpagez_none_p_kernel(tc, x_words, x_scales, w1, w2, ga
             return slice(HALF * h, HALF * (h + 1))
 
         xs = tile([P, T], U8, "xs")
-        nc.gpsimd.memset(xs[:].bitcast(I32), 0)
         pages = [tile([P, U], F32, f"page{u}") for u in range(PACK)]
 
         for q in range(4):
-            nc.sync.dma_start(xs[32 * q : 32 * q + 4, :].bitcast(I32), x_scales[0, 4 * q : 4 * q + 4, :].bitcast(I32))
-        by_row = x_scales[0].rearrange("(q r) n -> r q n", r=4)
-        for r in (2, 3):
-            nc.gpsimd.dma_start(xs[14 + r : P : 32, :].bitcast(I32), by_row[r].bitcast(I32))
+            rows = x_scales[0, 4 * q : 4 * q + 4, :].bitcast(I32)
+            nc.sync.dma_start(xs[32 * q : 32 * (q + 1), :].bitcast(I32), rows.unsqueeze(0).to_broadcast([8, 4, T // 4]))
         two_l = load_list(two, "two_l")
         offs_l = load_list(offs, "offs_l")
         xw = tile([P, T], U32, "xw")
@@ -56,17 +53,22 @@ def tile_picked_hkqoverhopdpagez_none_p_kernel(tc, x_words, x_scales, w1, w2, ga
         nc.sync.dma_start(w2_raw[:], w2.rearrange("(p j) c -> p j c", j=PACK))
         ga_t = tile([P, PACK], F32, "ga_t")
         gb_t = tile([P, PACK], F32, "gb_t")
-        nc.gpsimd.dma_start(ga_t[:], ga.rearrange("(p t) o -> p (t o)", t=PACK))
-        nc.gpsimd.dma_start(gb_t[:], gb.rearrange("(p t) o -> p (t o)", t=PACK))
+        nc.sync.dma_start(ga_t[:], ga.rearrange("(p t) o -> p (t o)", t=PACK))
+        nc.sync.dma_start(gb_t[:], gb.rearrange("(p t) o -> p (t o)", t=PACK))
         n3_l = load_list(n3, "n3_l")
         n4_l = load_list(n4, "n4_l")
         n1_l = load_list(n1, "n1_l")
-        n2_l = load_list(n2, "n2_l")
         w1_raw = tile([P, PACK, H], F32, "w1_raw")
         nc.sync.dma_start(w1_raw[:], w1.rearrange("(p j) c -> p j c", j=PACK))
+        n2_l = load_list(n2, "n2_l")
         n6_l = load_list(n6, "n6_l")
         n5_l = load_list(n5, "n5_l")
 
+        warm = tile([P, 1], F32, "warm")
+        a_win = tile([P, PACK, 2 * S], F32, "a_win")
+        zero = tile([P, 1], F32, "zero")
+        nc.gpsimd.memset(zero[:], 0.0)
+        nc.scalar.activation(warm[:], zero[:], ACT.Sigmoid)
         for u in range(PACK):
             (nc.vector if u < 2 else nc.gpsimd).memset(pages[u][:].bitcast(I32), 0)
 
@@ -88,7 +90,8 @@ def tile_picked_hkqoverhopdpagez_none_p_kernel(tc, x_words, x_scales, w1, w2, ga
         a_s = tile([P, S], U8, "a_s")
         nc.vector.tensor_copy(a_s[:].bitcast(I32), offs_s[:].bitcast(I32))
         for r in (2, 3):
-            nc.sync.dma_start(a_s[r:P:32, :].bitcast(I32), offs_s[14 + r : P : 32, :].bitcast(I32))
+            nc.sync.dma_start(a_s[r:P:32, :].bitcast(I32), offs_s[16 + r : P : 32, :].bitcast(I32))
+
 
         two_w = tile([P, V], U32, "two_w")
         nc.vector.tensor_copy(two_w[:], xw[:].indirect(two_l[:]))
@@ -110,17 +113,17 @@ def tile_picked_hkqoverhopdpagez_none_p_kernel(tc, x_words, x_scales, w1, w2, ga
             nc.tensor.matmul_mx(out=bank[:], lhsT=lhs[0][:, P * c : P * (c + 1)].bitcast(FP8X4), lhsT_scale=lhs[1][:, P * c : P * (c + 1)],
                                 rhs=rhs[0][:].bitcast(FP8X4), rhs_scale=rhs[1][:], start=True, stop=True)
 
-        w2_g = [cast_pair(w2_raw, u, f"w2_g{u}", nc.vector.tensor_copy if u == 0 else lambda o, i: nc.scalar.activation(o, i, ACT.Copy)) for u in range(2)]
+        w2_g = [cast_pair(w2_raw, u, f"w2_g{u}", nc.vector.tensor_copy if u == 0 else nc.scalar.copy) for u in range(2)]
         w2_q = [quantize(w2_g[u][:].rearrange("p t m j -> p (t m j)"), 2 * P, f"w2_q{u}") for u in range(2)]
         b_ps = [psum.tile([P, V], F32, name=f"b_ps{t}", tag=f"bank{t}") for t in range(PACK)]
         for t in range(PACK):
             product(b_ps[t], w2_q[t // 2], t % 2, (two_w, two_s))
 
-        b_win = [tile([P, V], F32, f"b_win{t}") for t in range(PACK)]
+        b_win = [tile([P, 2 * V], F32, f"b_win{t}") for t in range(PACK)]
         b_own = [tile([P, V], F32, f"b_own{t}") for t in range(PACK)]
         for t in range(PACK):
-            nc.scalar.copy(b_win[t][:], b_ps[t][:])
-            nc.sync.dma_start(b_own[t][:], b_win[t][:])
+            nc.scalar.copy(b_win[t][:, :V], b_ps[t][:])
+            nc.sync.dma_start(b_own[t][:], b_win[t][:, :V])
 
         w1_g = [cast_pair(w1_raw, u, f"w1_g{u}", nc.vector.tensor_copy) for u in range(2)]
         w1_q = [quantize(w1_g[u][:].rearrange("p t m j -> p (t m j)"), 2 * P, f"w1_q{u}") for u in range(2)]
@@ -128,34 +131,16 @@ def tile_picked_hkqoverhopdpagez_none_p_kernel(tc, x_words, x_scales, w1, w2, ga
         for t in range(PACK):
             product(a_ps[t], w1_q[t // 2], t % 2, (offs_w, a_s))
 
-        st = [tile([P, V], F32, f"st{t}") for t in range(PACK)]
+        st = [tile([P, 2 * V], F32, f"st{t}") for t in range(PACK)]
         sig = [tile([P, V], F32, f"sig{t}") for t in range(PACK)]
-        a_win = [tile([P, S], F32, f"a_win{t}") for t in range(PACK)]
-        g1 = [tile([P, S], F32, f"g1_{t}") for t in range(PACK)]
-        g2 = [tile([P, S], F32, f"g2_{t}") for t in range(PACK)]
-        big = [tile([P, S], F32, f"big{t}") for t in range(PACK)]
-        z_rows = tile([P, PACK, S], BF16, "z_rows")
+        g1, g2 = {}, {}
+        g1_on = ["g1_0", "st3", "sig1", "g1_3"]
+        g2_on = ["g2_0", "st2", "sig2", "sig3"]
+        big = tile([P, PACK, S], F32, "big")
         z2_rows = tile([P, PACK, V], BF16, "z2_rows")
 
         def a_evac(t):
-            nc.scalar.activation(a_win[t][:], a_ps[t][:], ACT.Copy, scale=ga_abs[:, t : t + 1])
-
-        def a_fetch(t, dst, lst, on_vector):
-            for h in range(2):
-                if on_vector:
-                    nc.vector.tensor_copy(dst[t][:, cols(h)], a_win[t][:].indirect(half(lst, h)))
-                else:
-                    nc.scalar.activation(dst[t][:, cols(h)], a_win[t][:].indirect(half(lst, h)), ACT.Copy)
-
-        def a_max(t, h):
-            nc.vector.tensor_tensor(big[t][:].rearrange("p (u m) -> p m u", u=PACK)[:, 64 * h : 64 * (h + 1), :],
-                                    g1[t][:, cols(h)].rearrange("p (m u) -> p m u", u=PACK),
-                                    g2[t][:, cols(h)].rearrange("p (m u) -> p m u", u=PACK), ALU.max)
-
-        def a_finish(t, u0, u1):
-            nc.vector.scalar_tensor_tensor(z_rows[:, t, :].rearrange("p (u m) -> p u m", u=PACK)[:, u0:u1, :],
-                                           a_ps[t][:].rearrange("p (m u) -> p u m", u=PACK)[:, u0:u1, :],
-                                           own[:, t : t + 1], big[t][:].rearrange("p (u m) -> p u m", u=PACK)[:, u0:u1, :], ALU.mult, ALU.add)
+            nc.scalar.activation(a_win[:, t, :S], a_ps[t][:], ACT.Copy, scale=own[:, t : t + 1])
 
         def interleave(rows, width, name, copy):
             grouped = tile([P, width, PACK], BF16, name)
@@ -163,59 +148,71 @@ def tile_picked_hkqoverhopdpagez_none_p_kernel(tc, x_words, x_scales, w1, w2, ga
             return grouped
 
         def b_sub(t):
-            for h in range(2):
-                nc.vector.tensor_tensor(st[t][:, cols(h)], b_win[t][:].indirect(half(n3_l, h)), b_own[t][:, cols(h)], ALU.subtract)
+            nc.vector.tensor_tensor(st[t][:, :V], b_win[t][:].indirect(n3_l[:]), b_own[t][:], ALU.subtract)
 
         def b_finish(t):
-            for h in range(2):
-                nc.scalar.activation(sig[t][:, cols(h)], st[t][:].indirect(half(n4_l, h)), ACT.Sigmoid)
+            nc.scalar.activation(sig[t][:], st[t][:].indirect(n4_l[:]), ACT.Sigmoid)
             nc.vector.scalar_tensor_tensor(z2_rows[:, t, :], sig[t][:], gb_s[:, t : t + 1], b_ps[t][:], ALU.mult, ALU.mult)
 
+        UNDO = -4.0 / 3.0
+        z_g = [tile([P, 2, P, PACK], BF16, f"z_g{k}") for k in range(2)]
+
+        def z_sum(k, m0, m1):
+            nc.vector.tensor_tensor(z_g[k][:].rearrange("p u m t -> p m t u")[:, m0:m1],
+                                    big[:].rearrange("p t (m u) -> p m t u", u=PACK)[:, m0:m1, :, 2 * k : 2 * k + 2],
+                                    a_win[:, :, :S].rearrange("p t (m u) -> p m t u", u=PACK)[:, m0:m1, :, 2 * k : 2 * k + 2], ALU.add)
+
         def a_tile(t):
-            a_fetch(t, g1, n1_l, t == PACK - 1)
-            a_fetch(t, g2, n2_l, False)
-            for h in range(2):
-                a_max(t, h)
-            a_finish(t, 0, PACK if t < PACK - 1 else 1)
+            g1[t] = tile([P, S], F32, f"g1_{t}", g1_on[t])
+            g2[t] = tile([P, S], F32, f"g2_{t}", g2_on[t])
+            if t < PACK - 1:
+                nc.scalar.activation(g1[t][:], a_win[:, t, :].indirect(n1_l[:]), ACT.Copy, scale=UNDO)
+                nc.scalar.activation(g2[t][:], a_win[:, t, :].indirect(n2_l[:]), ACT.Copy, scale=UNDO)
+                nc.vector.tensor_tensor(big[:, t, :], g1[t][:], g2[t][:], ALU.max)
+            else:
+                nc.vector.tensor_copy(g1[t][:], a_win[:, t, :].indirect(n1_l[:]))
+                for c0, c1 in ((0, 384), (384, S)):
+                    nc.scalar.activation(g2[t][:, c0:c1], a_win[:, t, :].indirect(n2_l[:, c0 // 16 : c1 // 16]), ACT.Copy, scale=UNDO)
+                    nc.vector.scalar_tensor_tensor(big[:, t, c0:c1], g1[t][:, c0:c1], UNDO, g2[t][:, c0:c1], ALU.mult, ALU.max)
+                    z_sum(0, c0 // PACK, c1 // PACK)
 
         for t in range(PACK):
             b_sub(t)
         a_evac(0)
         a_tile(0)
-        b_finish(0)
-        b_finish(1)
+        for t in range(PACK):
+            b_finish(t)
+        z2_g = interleave(z2_rows[:], V, "z2_g", nc.vector.tensor_copy)
+        z2_q = quantize(z2_g[:].rearrange("p c t -> p (c t)"), V, "z2_q")
         a_evac(1)
         a_evac(3)
         a_tile(1)
-        b_finish(2)
-        b_finish(3)
-        z2_g = interleave(z2_rows[:], V, "z2_g", nc.vector.tensor_copy)
-        z2_q = quantize(z2_g[:].rearrange("p c t -> p (c t)"), V, "z2_q")
         a_evac(2)
         a_tile(2)
         a_tile(3)
 
-        z_g0 = interleave(z_rows[:, :, 0:P], P, "z_g0", nc.vector.tensor_copy)
-        z_q0 = quantize(z_g0[:].rearrange("p c t -> p (c t)"), P, "z_q0")
         s_ps = [psum.tile([P, V], F32, name=f"s_ps{u}", tag=f"bank{u}") for u in range(PACK)]
-        product(s_ps[0], z_q0, 0, z2_q)
-        a_finish(PACK - 1, 1, PACK)
-        z_g1 = interleave(z_rows[:, :, P:S], S - P, "z_g1", nc.vector.tensor_copy)
-        z_q1 = quantize(z_g1[:].rearrange("p c t -> p (c t)"), S - P, "z_q1")
-        for u in range(1, PACK):
-            product(s_ps[u], z_q1, u - 1, z2_q)
+        for u in range(2):
+            product(s_ps[u], quantize(z_g[0][:, u].rearrange("p m t -> p (m t)"), P, f"z_q{u}"), 0, z2_q)
+        z_sum(1, 0, P)
+        z_q = quantize(z_g[1][:].rearrange("p u m t -> p (u m t)"), 2 * P, "z_q2")
+        for c in range(2):
+            product(s_ps[2 + c], z_q, c, z2_q)
 
         out_rows = out.rearrange("(p u) w -> u p w", u=PACK)
         for u in range(PACK):
-            pos = tile([P, V], F32, f"pos{u}")
-            nc.scalar.activation(pos[:], s_ps[u][:], ACT.Relu, scale=0.0625)
             s_own = tile([P, V], F32, f"s_own{u}")
+            if u > 0:
+                nc.scalar.activation(s_own[:], s_ps[u][:], ACT.Copy, scale=0.0625)
+            pos = tile([P, V], F32, f"pos{u}", "pos")
+            nc.scalar.activation(pos[:], s_ps[u][:], ACT.Relu, scale=0.0625)
             if u == 0:
                 nc.vector.tensor_scalar(s_own[:], s_ps[u][:], 0.0625, None, ALU.mult)
             neg = tile([P, V], F32, f"neg{u}")
             for h in range(2):
                 nc.scalar.activation(neg[:, cols(h)], pos[:].indirect(half(n6_l, h)), ACT.Copy, scale=-1.0)
+                if u == 0:
+                    nc.vector.tensor_tensor(pages[u][:].indirect(half(n5_l, h)), s_own[:, cols(h)], neg[:, cols(h)], ALU.add)
             if u > 0:
-                nc.scalar.activation(s_own[:], s_ps[u][:], ACT.Copy, scale=0.0625)
-            nc.vector.tensor_tensor(pages[u][:].indirect(n5_l[:]), s_own[:], neg[:], ALU.add)
+                nc.vector.tensor_tensor(pages[u][:].indirect(n5_l[:]), s_own[:], neg[:], ALU.add)
             nc.sync.dma_start(out_rows[u], pages[u][:])

@@ -15,11 +15,19 @@ ACT = mybir.ActivationFunctionType
 P = 128
 PACK = 4
 K, T, S, V, H, U = 512, 2048, 512, 512, 512, 1024
+GROUP = 16
+QUAD = 32
 HALF = 256
-FLOPS = 3 * 2 * 512 * 512 * 512
+OWN = -0.75
+UNDO_OWN = 1.0 / OWN
+S_SCALE = 0.0625
+LAST_CUT = 384
+FLOPS = 2 * K * H * S + 2 * K * H * V + 2 * H * S * V
 
 
-def tile_picked_hkqoverhopdpagez_none_p_kernel(tc, x_words, x_scales, w1, w2, ga, gb, offs, two, n1, n2, n3, n4, n5, n6, out):
+def tile_picked_hkqoverhopdpagez_none_p_kernel(
+    tc, x_words, x_scales, w1, w2, ga, gb, offs, two, n1, n2, n3, n4, n5, n6, out
+):
     nc = tc.nc
     with ExitStack() as ctx:
         keep = ctx.enter_context(tc.tile_pool(name="keep", bufs=1))
@@ -29,22 +37,23 @@ def tile_picked_hkqoverhopdpagez_none_p_kernel(tc, x_words, x_scales, w1, w2, ga
             return keep.tile(shape, dtype, name=name, tag=tag or name, align_bytes=64)
 
         def load_list(src, name):
-            t = keep.tile([P, S // 16], U16, name=name)
-            nc.sync.dma_start(t[:], src)
-            return t
-
-        def half(lst, h):
-            return lst[:, 16 * h : 16 * (h + 1)]
+            lst = keep.tile([P, S // GROUP], U16, name=name)
+            nc.sync.dma_start(lst[:], src)
+            return lst
 
         def cols(h):
             return slice(HALF * h, HALF * (h + 1))
 
+        def entries(lst, c):
+            return lst[:, c.start // GROUP : c.stop // GROUP]
+
         xs = tile([P, T], U8, "xs")
         pages = [tile([P, U], F32, f"page{u}") for u in range(PACK)]
-
-        for q in range(4):
+        for q in range(P // QUAD):
             rows = x_scales[0, 4 * q : 4 * q + 4, :].bitcast(I32)
-            nc.sync.dma_start(xs[32 * q : 32 * (q + 1), :].bitcast(I32), rows.unsqueeze(0).to_broadcast([8, 4, T // 4]))
+            nc.sync.dma_start(
+                xs[QUAD * q : QUAD * (q + 1), :].bitcast(I32), rows.unsqueeze(0).to_broadcast([QUAD // 4, 4, T // 4])
+            )
         two_l = load_list(two, "two_l")
         offs_l = load_list(offs, "offs_l")
         xw = tile([P, T], U32, "xw")
@@ -64,60 +73,74 @@ def tile_picked_hkqoverhopdpagez_none_p_kernel(tc, x_words, x_scales, w1, w2, ga
         n6_l = load_list(n6, "n6_l")
         n5_l = load_list(n5, "n5_l")
 
-        warm = tile([P, 1], F32, "warm")
-        a_win = tile([P, PACK, 2 * S], F32, "a_win")
-        zero = tile([P, 1], F32, "zero")
-        nc.gpsimd.memset(zero[:], 0.0)
-        nc.scalar.activation(warm[:], zero[:], ACT.Sigmoid)
         for u in range(PACK):
-            (nc.vector if u < 2 else nc.gpsimd).memset(pages[u][:].bitcast(I32), 0)
+            (nc.vector if u < PACK // 2 else nc.gpsimd).memset(pages[u][:].bitcast(I32), 0)
 
+        warm = tile([P, 1], F32, "warm")
+        nc.scalar.activation(warm[:], pages[0][:, 0:1], ACT.Sigmoid)
+
+        twice_pos = tile([P, PACK], F32, "twice_pos")
+        sign = tile([P, PACK], F32, "sign")
         ga_abs = tile([P, PACK], F32, "ga_abs")
-        pos2 = tile([P, PACK], F32, "pos2")
-        sgn = tile([P, PACK], F32, "sgn")
-        gb_s = tile([P, PACK], F32, "gb_s")
-        own = tile([P, PACK], F32, "own")
-        nc.gpsimd.tensor_scalar(pos2[:], ga_t[:], 0.0, 2.0, ALU.is_ge, ALU.mult)
-        nc.gpsimd.tensor_scalar(sgn[:], pos2[:], 1.0, -1.0, ALU.mult, ALU.add)
-        nc.gpsimd.tensor_tensor(ga_abs[:], ga_t[:], sgn[:], ALU.mult)
-        nc.gpsimd.tensor_tensor(gb_s[:], gb_t[:], sgn[:], ALU.mult)
-        nc.gpsimd.tensor_scalar(own[:], ga_abs[:], -0.75, 0.0, ALU.mult, ALU.add)
+        gb_signed = tile([P, PACK], F32, "gb_signed")
+        ga_own = tile([P, PACK], F32, "ga_own")
+        nc.gpsimd.tensor_scalar(twice_pos[:], ga_t[:], 0.0, 2.0, ALU.is_ge, ALU.mult)
+        nc.gpsimd.tensor_scalar(sign[:], twice_pos[:], 1.0, -1.0, ALU.mult, ALU.add)
+        nc.gpsimd.tensor_tensor(ga_abs[:], ga_t[:], sign[:], ALU.mult)
+        nc.gpsimd.tensor_tensor(gb_signed[:], gb_t[:], sign[:], ALU.mult)
+        nc.gpsimd.tensor_scalar(ga_own[:], ga_abs[:], OWN, 0.0, ALU.mult, ALU.add)
 
         two_s = tile([P, V], U8, "two_s")
         nc.vector.tensor_copy(two_s[:], xs[:].indirect(two_l[:]))
+        offs_picked = tile([P, S], U8, "offs_picked")
+        nc.vector.tensor_copy(offs_picked[:], xs[:].indirect(offs_l[:]))
         offs_s = tile([P, S], U8, "offs_s")
-        nc.vector.tensor_copy(offs_s[:], xs[:].indirect(offs_l[:]))
-        a_s = tile([P, S], U8, "a_s")
-        nc.vector.tensor_copy(a_s[:].bitcast(I32), offs_s[:].bitcast(I32))
+        nc.vector.tensor_copy(offs_s[:].bitcast(I32), offs_picked[:].bitcast(I32))
         for r in (2, 3):
-            nc.sync.dma_start(a_s[r:P:32, :].bitcast(I32), offs_s[16 + r : P : 32, :].bitcast(I32))
-
-
+            nc.sync.dma_start(offs_s[r:P:QUAD, :].bitcast(I32), offs_picked[GROUP + r : P : QUAD, :].bitcast(I32))
         two_w = tile([P, V], U32, "two_w")
         nc.vector.tensor_copy(two_w[:], xw[:].indirect(two_l[:]))
         offs_w = tile([P, S], U32, "offs_w")
         nc.vector.tensor_copy(offs_w[:], xw[:].indirect(offs_l[:]))
 
-        def cast_pair(raw, u, name, copy):
+        def round_weights(raw, pair, name, copy):
             grouped = tile([P, 2, P, PACK], BF16, name)
-            copy(grouped[:].rearrange("p t m j -> p m j t"), raw[:].rearrange("p j (m t) -> p m j t", t=PACK)[:, :, :, 2 * u : 2 * u + 2])
+            copy(
+                grouped[:].rearrange("p t m j -> p m j t"),
+                raw[:].rearrange("p j (m t) -> p m j t", t=PACK)[:, :, :, 2 * pair : 2 * pair + 2],
+            )
             return grouped
 
+        def mx_tiles(width, name):
+            return tile([P, width], U32, name + "_words"), tile([P, width], U8, name + "_scales")
+
+        def quantize_into(operand, c, flat):
+            nc.vector.quantize_mx(out=operand[0][:, c].bitcast(FP8X4), scales=operand[1][:, c], in_=flat)
+
         def quantize(flat, width, name):
-            codes = tile([P, width], U32, name + "_c")
-            scales = tile([P, width], U8, name + "_s")
-            nc.vector.quantize_mx(out=codes[:].bitcast(FP8X4), scales=scales[:], in_=flat)
-            return codes, scales
+            operand = mx_tiles(width, name)
+            quantize_into(operand, slice(0, width), flat)
+            return operand
 
-        def product(bank, lhs, c, rhs):
-            nc.tensor.matmul_mx(out=bank[:], lhsT=lhs[0][:, P * c : P * (c + 1)].bitcast(FP8X4), lhsT_scale=lhs[1][:, P * c : P * (c + 1)],
-                                rhs=rhs[0][:].bitcast(FP8X4), rhs_scale=rhs[1][:], start=True, stop=True)
+        def product(bank, lhs, block, rhs, c):
+            m = slice(P * block, P * (block + 1))
+            nc.tensor.matmul_mx(
+                out=bank[:],
+                lhsT=lhs[0][:, m].bitcast(FP8X4),
+                lhsT_scale=lhs[1][:, m],
+                rhs=rhs[0][:, c].bitcast(FP8X4),
+                rhs_scale=rhs[1][:, c],
+                start=True,
+                stop=True,
+            )
 
-        w2_g = [cast_pair(w2_raw, u, f"w2_g{u}", nc.vector.tensor_copy if u == 0 else nc.scalar.copy) for u in range(2)]
-        w2_q = [quantize(w2_g[u][:].rearrange("p t m j -> p (t m j)"), 2 * P, f"w2_q{u}") for u in range(2)]
+        every = slice(0, V)
+
+        w2_g = [round_weights(w2_raw, 0, "w2_g0", nc.vector.tensor_copy), round_weights(w2_raw, 1, "w2_g1", nc.scalar.copy)]
+        w2_q = [quantize(w2_g[i][:].rearrange("p t m j -> p (t m j)"), 2 * P, f"w2_q{i}") for i in range(2)]
         b_ps = [psum.tile([P, V], F32, name=f"b_ps{t}", tag=f"bank{t}") for t in range(PACK)]
         for t in range(PACK):
-            product(b_ps[t], w2_q[t // 2], t % 2, (two_w, two_s))
+            product(b_ps[t], w2_q[t // 2], t % 2, (two_w, two_s), every)
 
         b_win = [tile([P, 2 * V], F32, f"b_win{t}") for t in range(PACK)]
         b_own = [tile([P, V], F32, f"b_own{t}") for t in range(PACK)]
@@ -125,94 +148,136 @@ def tile_picked_hkqoverhopdpagez_none_p_kernel(tc, x_words, x_scales, w1, w2, ga
             nc.scalar.copy(b_win[t][:, :V], b_ps[t][:])
             nc.sync.dma_start(b_own[t][:], b_win[t][:, :V])
 
-        w1_g = [cast_pair(w1_raw, u, f"w1_g{u}", nc.vector.tensor_copy) for u in range(2)]
-        w1_q = [quantize(w1_g[u][:].rearrange("p t m j -> p (t m j)"), 2 * P, f"w1_q{u}") for u in range(2)]
-        a_ps = [psum.tile([P, S], F32, name=f"a_ps{t}", tag=f"bank{4 + t}") for t in range(PACK)]
+        w1_g = [round_weights(w1_raw, i, f"w1_g{i}", nc.vector.tensor_copy) for i in range(2)]
+        w1_q = [quantize(w1_g[i][:].rearrange("p t m j -> p (t m j)"), 2 * P, f"w1_q{i}") for i in range(2)]
+        a_ps = [psum.tile([P, S], F32, name=f"a_ps{t}", tag=f"bank{PACK + t}") for t in range(PACK)]
         for t in range(PACK):
-            product(a_ps[t], w1_q[t // 2], t % 2, (offs_w, a_s))
+            product(a_ps[t], w1_q[t // 2], t % 2, (offs_w, offs_s), every)
 
         st = [tile([P, 2 * V], F32, f"st{t}") for t in range(PACK)]
         sig = [tile([P, V], F32, f"sig{t}") for t in range(PACK)]
-        g1, g2 = {}, {}
-        g1_on = ["g1_0", "st3", "sig1", "g1_3"]
-        g2_on = ["g2_0", "st2", "sig2", "sig3"]
-        big = tile([P, PACK, S], F32, "big")
-        z2_rows = tile([P, PACK, V], BF16, "z2_rows")
+        a_win = tile([P, PACK, 2 * S], F32, "a_win")
+        larger = tile([P, PACK, S], F32, "larger")
+        z2_planes = tile([P, PACK, V], BF16, "z2_planes")
+        z_g = tile([P, PACK, P, PACK], BF16, "z_g")
 
-        def a_evac(t):
-            nc.scalar.activation(a_win[:, t, :S], a_ps[t][:], ACT.Copy, scale=own[:, t : t + 1])
-
-        def interleave(rows, width, name, copy):
-            grouped = tile([P, width, PACK], BF16, name)
-            copy(grouped[:].rearrange("p (c i) t -> p c t i", i=4), rows.rearrange("p t (c i) -> p c t i", i=4))
-            return grouped
-
-        def b_sub(t):
+        def st_plane(t):
             nc.vector.tensor_tensor(st[t][:, :V], b_win[t][:].indirect(n3_l[:]), b_own[t][:], ALU.subtract)
 
-        def b_finish(t):
+        def z2_plane(t):
             nc.scalar.activation(sig[t][:], st[t][:].indirect(n4_l[:]), ACT.Sigmoid)
-            nc.vector.scalar_tensor_tensor(z2_rows[:, t, :], sig[t][:], gb_s[:, t : t + 1], b_ps[t][:], ALU.mult, ALU.mult)
+            nc.vector.scalar_tensor_tensor(
+                z2_planes[:, t, :], sig[t][:], gb_signed[:, t : t + 1], b_ps[t][:], ALU.mult, ALU.mult
+            )
 
-        UNDO = -4.0 / 3.0
-        z_g = [tile([P, 2, P, PACK], BF16, f"z_g{k}") for k in range(2)]
+        def z2_words(h, copy):
+            grouped = tile([P, HALF, PACK], BF16, f"z2_g{h}")
+            copy(
+                grouped[:].rearrange("p (c i) t -> p c t i", i=4),
+                z2_planes[:, :, cols(h)].rearrange("p t (c i) -> p c t i", i=4),
+            )
+            quantize_into(z2_q, cols(h), grouped[:].rearrange("p c t -> p (c t)"))
 
-        def z_sum(k, m0, m1):
-            nc.vector.tensor_tensor(z_g[k][:].rearrange("p u m t -> p m t u")[:, m0:m1],
-                                    big[:].rearrange("p t (m u) -> p m t u", u=PACK)[:, m0:m1, :, 2 * k : 2 * k + 2],
-                                    a_win[:, :, :S].rearrange("p t (m u) -> p m t u", u=PACK)[:, m0:m1, :, 2 * k : 2 * k + 2], ALU.add)
+        def a_window(t):
+            nc.scalar.activation(a_win[:, t, :S], a_ps[t][:], ACT.Copy, scale=ga_own[:, t : t + 1])
 
-        def a_tile(t):
-            g1[t] = tile([P, S], F32, f"g1_{t}", g1_on[t])
-            g2[t] = tile([P, S], F32, f"g2_{t}", g2_on[t])
-            if t < PACK - 1:
-                nc.scalar.activation(g1[t][:], a_win[:, t, :].indirect(n1_l[:]), ACT.Copy, scale=UNDO)
-                nc.scalar.activation(g2[t][:], a_win[:, t, :].indirect(n2_l[:]), ACT.Copy, scale=UNDO)
-                nc.vector.tensor_tensor(big[:, t, :], g1[t][:], g2[t][:], ALU.max)
-            else:
-                nc.vector.tensor_copy(g1[t][:], a_win[:, t, :].indirect(n1_l[:]))
-                for c0, c1 in ((0, 384), (384, S)):
-                    nc.scalar.activation(g2[t][:, c0:c1], a_win[:, t, :].indirect(n2_l[:, c0 // 16 : c1 // 16]), ACT.Copy, scale=UNDO)
-                    nc.vector.scalar_tensor_tensor(big[:, t, c0:c1], g1[t][:, c0:c1], UNDO, g2[t][:, c0:c1], ALU.mult, ALU.max)
-                    z_sum(0, c0 // PACK, c1 // PACK)
+        def fetch_on_scalar(dst, t, offsets):
+            nc.scalar.activation(dst, a_win[:, t, :].indirect(offsets), ACT.Copy, scale=UNDO_OWN)
+
+        def fetch_on_vector(dst, t, offsets):
+            nc.vector.tensor_copy(dst, a_win[:, t, :].indirect(offsets))
+
+        def larger_plain(t, c, at_n1, at_n2):
+            nc.vector.tensor_tensor(larger[:, t, c], at_n1, at_n2, ALU.max)
+
+        def larger_mixed(t, c, at_n1_unscaled, at_n2):
+            nc.vector.scalar_tensor_tensor(larger[:, t, c], at_n1_unscaled, UNDO_OWN, at_n2, ALU.mult, ALU.max)
+
+        def fetch_tiles(t, n1_tag, n2_tag):
+            return tile([P, S], F32, f"at_n1_{t}", n1_tag), tile([P, S], F32, f"at_n2_{t}", n2_tag)
+
+        def larger_plane_on_scalar(t, n1_tag, n2_tag):
+            at_n1, at_n2 = fetch_tiles(t, n1_tag, n2_tag)
+            fetch_on_scalar(at_n1[:], t, n1_l[:])
+            fetch_on_scalar(at_n2[:], t, n2_l[:])
+            larger_plain(t, every, at_n1[:], at_n2[:])
+
+        def z_sum(pair, c):
+            m, u = slice(c.start // PACK, c.stop // PACK), slice(2 * pair, 2 * pair + 2)
+            nc.vector.tensor_tensor(
+                z_g[:].rearrange("p u m t -> p m t u")[:, m, :, u],
+                larger[:].rearrange("p t (m u) -> p m t u", u=PACK)[:, m, :, u],
+                a_win[:, :, :S].rearrange("p t (m u) -> p m t u", u=PACK)[:, m, :, u],
+                ALU.add,
+            )
 
         for t in range(PACK):
-            b_sub(t)
-        a_evac(0)
-        a_tile(0)
+            st_plane(t)
+        a_window(0)
+        larger_plane_on_scalar(0, None, None)
         for t in range(PACK):
-            b_finish(t)
-        z2_g = interleave(z2_rows[:], V, "z2_g", nc.vector.tensor_copy)
-        z2_q = quantize(z2_g[:].rearrange("p c t -> p (c t)"), V, "z2_q")
-        a_evac(1)
-        a_evac(3)
-        a_tile(1)
-        a_evac(2)
-        a_tile(2)
-        a_tile(3)
+            z2_plane(t)
+        z2_q = mx_tiles(V, "z2_q")
+        z2_words(0, nc.vector.tensor_copy)
+        a_window(1)
+        a_window(3)
+        larger_plane_on_scalar(1, "st3", "st2")
+        a_window(2)
 
-        s_ps = [psum.tile([P, V], F32, name=f"s_ps{u}", tag=f"bank{u}") for u in range(PACK)]
-        for u in range(2):
-            product(s_ps[u], quantize(z_g[0][:, u].rearrange("p m t -> p (m t)"), P, f"z_q{u}"), 0, z2_q)
-        z_sum(1, 0, P)
-        z_q = quantize(z_g[1][:].rearrange("p u m t -> p (u m t)"), 2 * P, "z_q2")
-        for c in range(2):
-            product(s_ps[2 + c], z_q, c, z2_q)
+        at_n1, at_n2 = fetch_tiles(2, "sig1", "sig2")
+        at_n1_first = tile([P, HALF], F32, "at_n1_first")
+        fetch_on_vector(at_n1_first[:], 2, entries(n1_l, cols(0)))
+        fetch_on_scalar(at_n1[:, cols(1)], 2, entries(n1_l, cols(1)))
+        fetch_on_scalar(at_n2[:], 2, n2_l[:])
+        larger_mixed(2, cols(0), at_n1_first[:], at_n2[:, cols(0)])
+        larger_plain(2, cols(1), at_n1[:, cols(1)], at_n2[:, cols(1)])
+
+        at_n1, at_n2 = fetch_tiles(3, None, "sig3")
+        fetch_on_vector(at_n1[:], 3, n1_l[:])
+        for c in (slice(0, LAST_CUT), slice(LAST_CUT, S)):
+            fetch_on_scalar(at_n2[:, c], 3, entries(n2_l, c))
+            larger_mixed(3, c, at_n1[:, c], at_n2[:, c])
+            z_sum(0, c)
+
+        z2_words(1, nc.scalar.copy)
+
+        z_q_first = quantize(z_g[:, 0].rearrange("p m t -> p (m t)"), P, "z_q_first")
+        s_first_ps = [psum.tile([P, HALF], F32, name=f"s_first_ps{h}", tag=f"bank{PACK * h}") for h in range(2)]
+        for h in range(2):
+            product(s_first_ps[h], z_q_first, 0, z2_q, cols(h))
+        z_sum(1, every)
+        z_q_rest = quantize(z_g[:, 1:].rearrange("p u m t -> p (u m t)"), (PACK - 1) * P, "z_q_rest")
+        s_ps = {u: psum.tile([P, V], F32, name=f"s_ps{u}", tag=f"bank{u}") for u in range(1, PACK)}
+        for u in range(1, PACK):
+            product(s_ps[u], z_q_rest, u - 1, z2_q, every)
 
         out_rows = out.rearrange("(p u) w -> u p w", u=PACK)
-        for u in range(PACK):
-            s_own = tile([P, V], F32, f"s_own{u}")
-            if u > 0:
-                nc.scalar.activation(s_own[:], s_ps[u][:], ACT.Copy, scale=0.0625)
-            pos = tile([P, V], F32, f"pos{u}", "pos")
-            nc.scalar.activation(pos[:], s_ps[u][:], ACT.Relu, scale=0.0625)
-            if u == 0:
-                nc.vector.tensor_scalar(s_own[:], s_ps[u][:], 0.0625, None, ALU.mult)
-            neg = tile([P, V], F32, f"neg{u}")
+
+        def page_tiles(u):
+            return tile([P, V], F32, f"s_own{u}"), tile([P, V], F32, f"pos{u}", "pos"), tile([P, V], F32, f"neg{u}")
+
+        def fetch_negative(neg, pos, h):
+            nc.scalar.activation(neg[:, cols(h)], pos[:].indirect(entries(n6_l, cols(h))), ACT.Copy, scale=-1.0)
+
+        def scatter(u, c, s_own, neg):
+            nc.vector.tensor_tensor(pages[u][:].indirect(entries(n5_l, c)), s_own[:, c], neg[:, c], ALU.add)
+
+        s_own, pos, neg = page_tiles(0)
+        for h in range(2):
+            nc.scalar.activation(pos[:, cols(h)], s_first_ps[h][:], ACT.Relu, scale=S_SCALE)
+        nc.vector.tensor_scalar(s_own[:, cols(0)], s_first_ps[0][:], S_SCALE, None, ALU.mult)
+        fetch_negative(neg, pos, 0)
+        scatter(0, cols(0), s_own, neg)
+        fetch_negative(neg, pos, 1)
+        nc.scalar.activation(s_own[:, cols(1)], s_first_ps[1][:], ACT.Copy, scale=S_SCALE)
+        scatter(0, cols(1), s_own, neg)
+        nc.sync.dma_start(out_rows[0], pages[0][:])
+
+        for u in range(1, PACK):
+            s_own, pos, neg = page_tiles(u)
+            nc.scalar.activation(s_own[:], s_ps[u][:], ACT.Copy, scale=S_SCALE)
+            nc.scalar.activation(pos[:], s_ps[u][:], ACT.Relu, scale=S_SCALE)
             for h in range(2):
-                nc.scalar.activation(neg[:, cols(h)], pos[:].indirect(half(n6_l, h)), ACT.Copy, scale=-1.0)
-                if u == 0:
-                    nc.vector.tensor_tensor(pages[u][:].indirect(half(n5_l, h)), s_own[:, cols(h)], neg[:, cols(h)], ALU.add)
-            if u > 0:
-                nc.vector.tensor_tensor(pages[u][:].indirect(n5_l[:]), s_own[:], neg[:], ALU.add)
+                fetch_negative(neg, pos, h)
+            scatter(u, every, s_own, neg)
             nc.sync.dma_start(out_rows[u], pages[u][:])

from contextlib import ExitStack

import concourse.mybir as mybir

F32 = mybir.dt.float32
BF16 = mybir.dt.bfloat16
I32 = mybir.dt.int32
U32 = mybir.dt.uint32
U16 = mybir.dt.uint16
U8 = mybir.dt.uint8
FP8X4 = mybir.dt.float8_e4m3fn_x4
ALU = mybir.AluOpType
ACT = mybir.ActivationFunctionType

P = 128
PACK = 4
K, T, S, V, H, U = 512, 2048, 512, 512, 512, 1024
GROUP = 16
QUAD = 32
HALF = 256
OWN = -0.75
UNDO_OWN = 1.0 / OWN
S_SCALE = 0.0625
LAST_CUT = 384
FLOPS = 2 * K * H * S + 2 * K * H * V + 2 * H * S * V


def tile_picked_hkqoverhopdpagez_none_p_kernel(
    tc, x_words, x_scales, w1, w2, ga, gb, offs, two, n1, n2, n3, n4, n5, n6, out
):
    nc = tc.nc
    with ExitStack() as ctx:
        keep = ctx.enter_context(tc.tile_pool(name="keep", bufs=1))
        psum = ctx.enter_context(tc.psum_pool(name="psum", bufs=1))

        def tile(shape, dtype, name, tag=None):
            return keep.tile(shape, dtype, name=name, tag=tag or name, align_bytes=64)

        def load_list(src, name):
            lst = keep.tile([P, S // GROUP], U16, name=name)
            nc.sync.dma_start(lst[:], src)
            return lst

        def cols(h):
            return slice(HALF * h, HALF * (h + 1))

        def entries(lst, c):
            return lst[:, c.start // GROUP : c.stop // GROUP]

        xs = tile([P, T], U8, "xs")
        pages = [tile([P, U], F32, f"page{u}") for u in range(PACK)]
        for q in range(P // QUAD):
            rows = x_scales[0, 4 * q : 4 * q + 4, :].bitcast(I32)
            nc.sync.dma_start(
                xs[QUAD * q : QUAD * (q + 1), :].bitcast(I32), rows.unsqueeze(0).to_broadcast([QUAD // 4, 4, T // 4])
            )
        two_l = load_list(two, "two_l")
        offs_l = load_list(offs, "offs_l")
        xw = tile([P, T], U32, "xw")
        nc.sync.dma_start(xw[:].bitcast(I32), x_words[0].rearrange("p n t -> p (n t)").bitcast(I32))
        w2_raw = tile([P, PACK, H], F32, "w2_raw")
        nc.sync.dma_start(w2_raw[:], w2.rearrange("(p j) c -> p j c", j=PACK))
        ga_t = tile([P, PACK], F32, "ga_t")
        gb_t = tile([P, PACK], F32, "gb_t")
        nc.sync.dma_start(ga_t[:], ga.rearrange("(p t) o -> p (t o)", t=PACK))
        nc.sync.dma_start(gb_t[:], gb.rearrange("(p t) o -> p (t o)", t=PACK))
        n3_l = load_list(n3, "n3_l")
        n4_l = load_list(n4, "n4_l")
        n1_l = load_list(n1, "n1_l")
        w1_raw = tile([P, PACK, H], F32, "w1_raw")
        nc.sync.dma_start(w1_raw[:], w1.rearrange("(p j) c -> p j c", j=PACK))
        n2_l = load_list(n2, "n2_l")
        n6_l = load_list(n6, "n6_l")
        n5_l = load_list(n5, "n5_l")

        for u in range(PACK):
            (nc.vector if u < PACK // 2 else nc.gpsimd).memset(pages[u][:].bitcast(I32), 0)

        warm = tile([P, 1], F32, "warm")
        nc.scalar.activation(warm[:], pages[0][:, 0:1], ACT.Sigmoid)

        twice_pos = tile([P, PACK], F32, "twice_pos")
        sign = tile([P, PACK], F32, "sign")
        ga_abs = tile([P, PACK], F32, "ga_abs")
        gb_signed = tile([P, PACK], F32, "gb_signed")
        ga_own = tile([P, PACK], F32, "ga_own")
        nc.gpsimd.tensor_scalar(twice_pos[:], ga_t[:], 0.0, 2.0, ALU.is_ge, ALU.mult)
        nc.gpsimd.tensor_scalar(sign[:], twice_pos[:], 1.0, -1.0, ALU.mult, ALU.add)
        nc.gpsimd.tensor_tensor(ga_abs[:], ga_t[:], sign[:], ALU.mult)
        nc.gpsimd.tensor_tensor(gb_signed[:], gb_t[:], sign[:], ALU.mult)
        nc.gpsimd.tensor_scalar(ga_own[:], ga_abs[:], OWN, 0.0, ALU.mult, ALU.add)

        two_s = tile([P, V], U8, "two_s")
        nc.vector.tensor_copy(two_s[:], xs[:].indirect(two_l[:]))
        offs_picked = tile([P, S], U8, "offs_picked")
        nc.vector.tensor_copy(offs_picked[:], xs[:].indirect(offs_l[:]))
        offs_s = tile([P, S], U8, "offs_s")
        nc.vector.tensor_copy(offs_s[:].bitcast(I32), offs_picked[:].bitcast(I32))
        for r in (2, 3):
            nc.sync.dma_start(offs_s[r:P:QUAD, :].bitcast(I32), offs_picked[GROUP + r : P : QUAD, :].bitcast(I32))
        two_w = tile([P, V], U32, "two_w")
        nc.vector.tensor_copy(two_w[:], xw[:].indirect(two_l[:]))
        offs_w = tile([P, S], U32, "offs_w")
        nc.vector.tensor_copy(offs_w[:], xw[:].indirect(offs_l[:]))

        def round_weights(raw, pair, name, copy):
            grouped = tile([P, 2, P, PACK], BF16, name)
            copy(
                grouped[:].rearrange("p t m j -> p m j t"),
                raw[:].rearrange("p j (m t) -> p m j t", t=PACK)[:, :, :, 2 * pair : 2 * pair + 2],
            )
            return grouped

        def mx_tiles(width, name):
            return tile([P, width], U32, name + "_words"), tile([P, width], U8, name + "_scales")

        def quantize_into(operand, c, flat):
            nc.vector.quantize_mx(out=operand[0][:, c].bitcast(FP8X4), scales=operand[1][:, c], in_=flat)

        def quantize(flat, width, name):
            operand = mx_tiles(width, name)
            quantize_into(operand, slice(0, width), flat)
            return operand

        def product(bank, lhs, block, rhs, c):
            m = slice(P * block, P * (block + 1))
            nc.tensor.matmul_mx(
                out=bank[:],
                lhsT=lhs[0][:, m].bitcast(FP8X4),
                lhsT_scale=lhs[1][:, m],
                rhs=rhs[0][:, c].bitcast(FP8X4),
                rhs_scale=rhs[1][:, c],
                start=True,
                stop=True,
            )

        every = slice(0, V)

        w2_g = [round_weights(w2_raw, 0, "w2_g0", nc.vector.tensor_copy), round_weights(w2_raw, 1, "w2_g1", nc.scalar.copy)]
        w2_q = [quantize(w2_g[i][:].rearrange("p t m j -> p (t m j)"), 2 * P, f"w2_q{i}") for i in range(2)]
        b_ps = [psum.tile([P, V], F32, name=f"b_ps{t}", tag=f"bank{t}") for t in range(PACK)]
        for t in range(PACK):
            product(b_ps[t], w2_q[t // 2], t % 2, (two_w, two_s), every)

        b_win = [tile([P, 2 * V], F32, f"b_win{t}") for t in range(PACK)]
        b_own = [tile([P, V], F32, f"b_own{t}") for t in range(PACK)]
        for t in range(PACK):
            nc.scalar.copy(b_win[t][:, :V], b_ps[t][:])
            nc.sync.dma_start(b_own[t][:], b_win[t][:, :V])

        w1_g = [round_weights(w1_raw, i, f"w1_g{i}", nc.vector.tensor_copy) for i in range(2)]
        w1_q = [quantize(w1_g[i][:].rearrange("p t m j -> p (t m j)"), 2 * P, f"w1_q{i}") for i in range(2)]
        a_ps = [psum.tile([P, S], F32, name=f"a_ps{t}", tag=f"bank{PACK + t}") for t in range(PACK)]
        for t in range(PACK):
            product(a_ps[t], w1_q[t // 2], t % 2, (offs_w, offs_s), every)

        st = [tile([P, 2 * V], F32, f"st{t}") for t in range(PACK)]
        sig = [tile([P, V], F32, f"sig{t}") for t in range(PACK)]
        a_win = tile([P, PACK, 2 * S], F32, "a_win")
        larger = tile([P, PACK, S], F32, "larger")
        z2_planes = tile([P, PACK, V], BF16, "z2_planes")
        z_g = tile([P, PACK, P, PACK], BF16, "z_g")

        def st_plane(t):
            nc.vector.tensor_tensor(st[t][:, :V], b_win[t][:].indirect(n3_l[:]), b_own[t][:], ALU.subtract)

        def z2_plane(t):
            nc.scalar.activation(sig[t][:], st[t][:].indirect(n4_l[:]), ACT.Sigmoid)
            nc.vector.scalar_tensor_tensor(
                z2_planes[:, t, :], sig[t][:], gb_signed[:, t : t + 1], b_ps[t][:], ALU.mult, ALU.mult
            )

        def z2_words(h, copy):
            grouped = tile([P, HALF, PACK], BF16, f"z2_g{h}")
            copy(
                grouped[:].rearrange("p (c i) t -> p c t i", i=4),
                z2_planes[:, :, cols(h)].rearrange("p t (c i) -> p c t i", i=4),
            )
            quantize_into(z2_q, cols(h), grouped[:].rearrange("p c t -> p (c t)"))

        def a_window(t):
            nc.scalar.activation(a_win[:, t, :S], a_ps[t][:], ACT.Copy, scale=ga_own[:, t : t + 1])

        def fetch_on_scalar(dst, t, offsets):
            nc.scalar.activation(dst, a_win[:, t, :].indirect(offsets), ACT.Copy, scale=UNDO_OWN)

        def fetch_on_vector(dst, t, offsets):
            nc.vector.tensor_copy(dst, a_win[:, t, :].indirect(offsets))

        def larger_plain(t, c, at_n1, at_n2):
            nc.vector.tensor_tensor(larger[:, t, c], at_n1, at_n2, ALU.max)

        def larger_mixed(t, c, at_n1_unscaled, at_n2):
            nc.vector.scalar_tensor_tensor(larger[:, t, c], at_n1_unscaled, UNDO_OWN, at_n2, ALU.mult, ALU.max)

        def fetch_tiles(t, n1_tag, n2_tag):
            return tile([P, S], F32, f"at_n1_{t}", n1_tag), tile([P, S], F32, f"at_n2_{t}", n2_tag)

        def larger_plane_on_scalar(t, n1_tag, n2_tag):
            at_n1, at_n2 = fetch_tiles(t, n1_tag, n2_tag)
            fetch_on_scalar(at_n1[:], t, n1_l[:])
            fetch_on_scalar(at_n2[:], t, n2_l[:])
            larger_plain(t, every, at_n1[:], at_n2[:])

        def z_sum(pair, c):
            m, u = slice(c.start // PACK, c.stop // PACK), slice(2 * pair, 2 * pair + 2)
            nc.vector.tensor_tensor(
                z_g[:].rearrange("p u m t -> p m t u")[:, m, :, u],
                larger[:].rearrange("p t (m u) -> p m t u", u=PACK)[:, m, :, u],
                a_win[:, :, :S].rearrange("p t (m u) -> p m t u", u=PACK)[:, m, :, u],
                ALU.add,
            )

        for t in range(PACK):
            st_plane(t)
        a_window(0)
        larger_plane_on_scalar(0, None, None)
        for t in range(PACK):
            z2_plane(t)
        z2_q = mx_tiles(V, "z2_q")
        z2_words(0, nc.vector.tensor_copy)
        a_window(1)
        a_window(3)
        larger_plane_on_scalar(1, "st3", "st2")
        a_window(2)

        at_n1, at_n2 = fetch_tiles(2, "sig1", "sig2")
        at_n1_first = tile([P, HALF], F32, "at_n1_first")
        fetch_on_vector(at_n1_first[:], 2, entries(n1_l, cols(0)))
        fetch_on_scalar(at_n1[:, cols(1)], 2, entries(n1_l, cols(1)))
        fetch_on_scalar(at_n2[:], 2, n2_l[:])
        larger_mixed(2, cols(0), at_n1_first[:], at_n2[:, cols(0)])
        larger_plain(2, cols(1), at_n1[:, cols(1)], at_n2[:, cols(1)])

        at_n1, at_n2 = fetch_tiles(3, None, "sig3")
        fetch_on_vector(at_n1[:], 3, n1_l[:])
        for c in (slice(0, LAST_CUT), slice(LAST_CUT, S)):
            fetch_on_scalar(at_n2[:, c], 3, entries(n2_l, c))
            larger_mixed(3, c, at_n1[:, c], at_n2[:, c])
            z_sum(0, c)

        z2_words(1, nc.scalar.copy)

        z_q_first = quantize(z_g[:, 0].rearrange("p m t -> p (m t)"), P, "z_q_first")
        s_first_ps = [psum.tile([P, HALF], F32, name=f"s_first_ps{h}", tag=f"bank{PACK * h}") for h in range(2)]
        for h in range(2):
            product(s_first_ps[h], z_q_first, 0, z2_q, cols(h))
        z_sum(1, every)
        z_q_rest = quantize(z_g[:, 1:].rearrange("p u m t -> p (u m t)"), (PACK - 1) * P, "z_q_rest")
        s_ps = {u: psum.tile([P, V], F32, name=f"s_ps{u}", tag=f"bank{u}") for u in range(1, PACK)}
        for u in range(1, PACK):
            product(s_ps[u], z_q_rest, u - 1, z2_q, every)

        out_rows = out.rearrange("(p u) w -> u p w", u=PACK)

        def page_tiles(u):
            return tile([P, V], F32, f"s_own{u}"), tile([P, V], F32, f"pos{u}", "pos"), tile([P, V], F32, f"neg{u}")

        def fetch_negative(neg, pos, h):
            nc.scalar.activation(neg[:, cols(h)], pos[:].indirect(entries(n6_l, cols(h))), ACT.Copy, scale=-1.0)

        def scatter(u, c, s_own, neg):
            nc.vector.tensor_tensor(pages[u][:].indirect(entries(n5_l, c)), s_own[:, c], neg[:, c], ALU.add)

        s_own, pos, neg = page_tiles(0)
        for h in range(2):
            nc.scalar.activation(pos[:, cols(h)], s_first_ps[h][:], ACT.Relu, scale=S_SCALE)
        nc.vector.tensor_scalar(s_own[:, cols(0)], s_first_ps[0][:], S_SCALE, None, ALU.mult)
        fetch_negative(neg, pos, 0)
        scatter(0, cols(0), s_own, neg)
        fetch_negative(neg, pos, 1)
        nc.scalar.activation(s_own[:, cols(1)], s_first_ps[1][:], ACT.Copy, scale=S_SCALE)
        scatter(0, cols(1), s_own, neg)
        nc.sync.dma_start(out_rows[0], pages[0][:])

        for u in range(1, PACK):
            s_own, pos, neg = page_tiles(u)
            nc.scalar.activation(s_own[:], s_ps[u][:], ACT.Copy, scale=S_SCALE)
            nc.scalar.activation(pos[:], s_ps[u][:], ACT.Relu, scale=S_SCALE)
            for h in range(2):
                fetch_negative(neg, pos, h)
            scatter(u, every, s_own, neg)
            nc.sync.dma_start(out_rows[u], pages[u][:])
